import numpy as np, ml_dtypes
CORES = [113,118,241,246]
N = 4
import mx_ref
NC, G = 128, 2
C = np.float32(0.0145)
BF = ml_dtypes.bfloat16
def cut(t, i, w=512):
    return t[:, w * i:w * i + w]
def tile(rs):
    return np.stack(rs, axis=2).reshape(128, -1).astype(BF)
def layer(w, X):
    out = []
    for i in range(G):
        for t in range(len(X)):
            p = mx_ref.matmul(mx_ref.quantize(cut(w, len(X) * i + t)), X[t])
            z = p if t == 0 else z + p
        out.append(z)
    return out
def act(Z):
    return [np.maximum(s * z, 0) * C for z in Z for s in (1, -1)]
def setup_inputs(rng):
    def f(*shape):
        return mx_ref.flush((rng.standard_normal(shape, dtype=np.float32) * np.exp2(rng.integers(-2, 3, shape[:-1] + (1,)))).astype(BF))
    return {"x": f(N, 128, 4 * NC), "w1": f(N, 128, G * N * 512), "w2": f(N, 128, 2 * 512)}
def setup_inputs_blocks(rng):
    d = setup_inputs(rng)
    for k in ("x", "w1", "w2"): d[k] = mx_ref.spread(d[k], rng, 4)
    return d
def setup_inputs_wide(rng):
    d = setup_inputs(rng)
    for k in ("x", "w1", "w2"): d[k] = mx_ref.flush((d[k].astype(np.float32) * np.exp2(rng.integers(-6, 7, (N, 1, 1))).astype(np.float32)).astype(BF))
    return d
def reference(x, w1, w2, own=None):
    X = [mx_ref.quantize(x[j]) for j in range(N)]
    h = np.stack([tile(act(layer(w1[r], X))) for r in range(N)])
    use = h if own is None else own["h"]
    H = [mx_ref.quantize(use[j]) for j in range(N)]
    y = np.zeros((N, 128, NC), np.float32)
    for r in range(N):
        y[r] = mx_ref.matmul(mx_ref.quantize(cut(w2[r], 0)), H[r]) + mx_ref.matmul(mx_ref.quantize(cut(w2[r], 1)), H[(r + 1) % N])
    return {"h": h, "y": y}

from concourse.bass import DstId, RemoteDMATransfer
from concourse.mybir import dt, AluOpType, ActivationFunctionType

N = 4
NC = 128
G = 2
C = 0.0145

SCRATCH = {
    "xt": ("sbuf", [128, 4 * NC], "bfloat16"),
    "w1t": ("sbuf", [128, G * N * 512], "bfloat16"),
    "w2t": ("sbuf", [128, 2 * 512], "bfloat16"),
    "ht": ("sbuf", [128, 4 * NC], "bfloat16"),
    "yt": ("sbuf", [128, NC], "float32"),
    "qx": ("sbuf", [128, N * NC], "float8_e4m3fn_x4"),
    "px": ("sbuf", [128, N * NC], "uint8"),
    "qw1": ("sbuf", [128, G * N * 128], "float8_e4m3fn_x4"),
    "pw1": ("sbuf", [128, G * N * 128], "uint8"),
    "qw2": ("sbuf", [128, 2 * 128], "float8_e4m3fn_x4"),
    "pw2": ("sbuf", [128, 2 * 128], "uint8"),
    "qh": ("sbuf", [128, 2 * NC], "float8_e4m3fn_x4"),
    "ph": ("sbuf", [128, 2 * NC], "uint8"),
    "ps": ("psum", [128, 3 * 512], "float32"),
}
SEMAPHORES = ["ld_x", "ld_w1_0", "ld_w1_1", "ld_w2", "st_h", "st_y",
              "q_x", "q_w1_0", "q_w1_1", "q_w2", "q_h",
              "xa0", "xa1", "xa2", "xa3", "ha",
              "z0", "z1", "h_done", "y_sum", "y_copied",
              "x_issued", "h_issued", "sent"]


def rank_program(g, core, T, topo):
    r = T.rank_of(core)
    if r is None:
        return
    cores = list(T.cores)
    S = T.sem
    Relu = ActivationFunctionType.Relu

    def same_chip(a, b):
        return topo.host(a) == topo.host(b) and topo.chip(a) == topo.chip(b)

    def count(mask):
        return bin(mask).count("1")

    def x_plan(s):
        src = cores[s]
        near = [d for d in range(N) if d != s and same_chip(src, cores[d])]
        far = [d for d in range(N) if d != s and not same_chip(src, cores[d])]
        far.sort(key=lambda d: same_chip(cores[d], cores[(d - 1) % N]))
        far_mask = topo.mask(src, cores[far[0]])
        for d in far:
            far_mask &= topo.mask(src, cores[d])
        waves = [[(d, far_mask)] for d in far]
        for d in near:
            waves[0].append((d, topo.mask(src, cores[d]) & ~far_mask))
        return waves

    def h_mask(s):
        return topo.mask(cores[s], cores[(s - 1) % N])

    sent = [0]

    def send(src, dst, dests, sem):
        trs = []
        for d, m in dests:
            rid, pid = topo.addr(cores[d], core)
            trs.append(RemoteDMATransfer(dst_ids=[DstId(rid=rid, pnc=pid)], dma_engine_mask=m, remote_sem=sem,
                                         src=src(), dst=dst()))
            sent[0] += count(m)
        g.remote_dma_fused(trs, local_sem=S.sent)

    def slot(j):
        return slice(NC * j, NC * j + NC)

    sy = g.sync
    sy.dma_start(T.xt[:], T.x[:]).then_inc(S.ld_x, 16)
    half = N * 512
    for i in range(G):
        sy.dma_start(T.w1t[:, half * i:half * (i + 1)], T.w1[:, half * i:half * (i + 1)]).then_inc(S["ld_w1_%d" % i], 16)
    sy.wait_ge(S.x_issued, 1)
    sy.dma_start(T.w2t[:], T.w2[:]).then_inc(S.ld_w2, 16)
    sy.wait_ge(S.h_done, 4)
    sy.wait_ge(S.h_issued, 1)
    sy.dma_start(T.h[:], T.ht[:]).then_inc(S.st_h, 16)
    sy.wait_ge(S.y_copied, 1)
    sy.dma_start(T.y[:], T.yt[:]).then_inc(S.st_y, 16)
    sy.wait_ge(S.st_h, 16)
    sy.wait_ge(S.st_y, 16)

    g.wait_ge(S.q_x, 1)
    for wave in x_plan(r):
        send(lambda: T.qx[:, slot(r)].bitcast(dt.uint8), lambda: T.qx[:, slot(r)].bitcast(dt.uint8), wave, S["xa%d" % r])
        send(lambda: T.px[:, slot(r)], lambda: T.px[:, slot(r)], wave, S["xa%d" % r])
    g.sem_inc(S.x_issued, 1)
    g.wait_ge(S.q_h, 1)
    to = [((r - 1) % N, h_mask(r))]
    send(lambda: T.qh[:, slot(0)].bitcast(dt.uint8), lambda: T.qh[:, slot(1)].bitcast(dt.uint8), to, S.ha)
    send(lambda: T.ph[:, slot(0)], lambda: T.ph[:, slot(1)], to, S.ha)
    g.sem_inc(S.h_issued, 1)
    g.wait_ge(S.sent, sent[0])

    ve = g.vector
    ve.wait_ge(S.ld_x, 16)
    ve.quantize_mx(T.qx[:, slot(r)], T.px[:, slot(r)], T.xt[:]).then_inc(S.q_x, 1)
    for i in range(G):
        ve.wait_ge(S["ld_w1_%d" % i], 16)
        ve.quantize_mx(T.qw1[:, 512 * i:512 * (i + 1)], T.pw1[:, 512 * i:512 * (i + 1)],
                       T.w1t[:, half * i:half * (i + 1)]).then_inc(S["q_w1_%d" % i], 1)
    ve.wait_ge(S.z0, 1)
    ve.tensor_scalar(T.ht[:, 0:4 * NC:4], T.ps[:, 0:NC], 0.0, C, AluOpType.max, AluOpType.mult).then_inc(S.h_done, 1)
    ve.tensor_scalar(T.ht[:, 1:4 * NC:4], T.ps[:, 0:NC], -C, 0.0, AluOpType.mult, AluOpType.max).then_inc(S.h_done, 1)
    ve.wait_ge(S.h_done, 4)
    ve.quantize_mx(T.qh[:, slot(0)], T.ph[:, slot(0)], T.ht[:]).then_inc(S.q_h, 1)
    ve.wait_ge(S.ld_w2, 16)
    ve.quantize_mx(T.qw2[:], T.pw2[:], T.w2t[:]).then_inc(S.q_w2, 1)
    ve.wait_ge(S.y_sum, 1)
    ve.tensor_copy(T.yt[:], T.ps[:, 1024:1024 + NC]).then_inc(S.y_copied, 1)

    sc = g.scalar
    sc.wait_ge(S.z1, 1)
    sc.activation(T.ht[:, 2:4 * NC:4], T.ps[:, 512:512 + NC], Relu, scale=C).then_inc(S.h_done, 1)
    sc.activation(T.ht[:, 3:4 * NC:4], T.ps[:, 512:512 + NC], Relu, scale=-C).then_inc(S.h_done, 1)

    te = g.tensor
    peers = [j for j in range(N) if j != r]
    peers.sort(key=lambda j: not same_chip(core, cores[j]))
    order = [r] + peers
    te.wait_ge(S.q_x, 1)
    for n, j in enumerate(order):
        if j != r:
            mine = [m for wave in x_plan(j) for d, m in wave if d == r]
            te.wait_ge(S["xa%d" % j], 2 * count(mine[0]))
        for i in range(G):
            if n == 0:
                te.wait_ge(S["q_w1_%d" % i], 1)
            k = N * i + j
            mm = te.matmul_mx(T.ps[:, 512 * i:512 * i + NC], T.qw1[:, slot(k)], T.pw1[:, slot(k)],
                              T.qx[:, slot(j)], T.px[:, slot(j)], n == 0, n == N - 1)
            if n == N - 1:
                mm.then_inc(S["z%d" % i], 1)
    te.wait_ge(S.q_h, 1)
    te.wait_ge(S.q_w2, 1)
    te.matmul_mx(T.ps[:, 1024:1024 + NC], T.qw2[:, slot(0)], T.pw2[:, slot(0)], T.qh[:, slot(0)], T.ph[:, slot(0)], True, False)
    te.wait_ge(S.ha, 2 * count(h_mask((r + 1) % N)))
    te.matmul_mx(T.ps[:, 1024:1024 + NC], T.qw2[:, slot(1)], T.pw2[:, slot(1)], T.qh[:, slot(1)], T.ph[:, slot(1)],
                 False, True).then_inc(S.y_sum, 1)
